import numpy as np
import ml_dtypes


def mxq(x, axis, fmt="e4m3"):
    dtype, down = {"e4m3": (ml_dtypes.float8_e4m3fn, 7), "e5m2": (ml_dtypes.float8_e5m2, 14)}[fmt]
    v = np.moveaxis(np.asarray(x, np.float32).astype(ml_dtypes.bfloat16).astype(np.float64), axis, -1)
    blocks = v.reshape(v.shape[:-1] + (-1, 32))
    amax = np.abs(blocks).max(-1, keepdims=True)
    byte = np.maximum(np.where(amax > 0, np.frexp(amax)[1] - 1 + 127, 0) - down, 1)
    scale = np.exp2(byte - 127.0)
    codes = (blocks / scale).astype(np.float32).astype(dtype).astype(np.float64)
    return np.moveaxis((codes * scale).reshape(v.shape), -1, axis)


WIDE = False


def mx_kscale(k):
    if not WIDE:
        return np.ones(k)
    levels = np.array([10, -10, 5, -5, 0])
    if k % 512:
        return np.exp2(np.random.permutation(np.resize(levels, k // 32))).repeat(32)
    a = np.empty((k // 512, 16))
    for p in range(k // 512):
        a[p, :8] = np.random.permutation(np.resize(levels, 8))
        for g in range(8):
            far = levels[np.abs(levels - a[p, g]) >= 10]
            a[p, g + 8] = far[np.random.randint(len(far))]
    return np.exp2(a.ravel()).repeat(32)


def f64(x):
    return np.asarray(x).astype(np.float64)


def striped(idx):
    return np.tile(idx.reshape(-1, 16).T, (8, 1)).astype(np.uint16)


def unstriped(offs):
    return offs[:16].T.reshape(-1).astype(np.int64)


def striped8(idx):
    return np.concatenate([x.reshape(-1, 16).T for x in idx]).astype(np.uint16)


def runs(offs, k):
    lists = np.stack([offs[16 * r : 16 * r + 16].T.reshape(-1) for r in range(8)]).astype(np.int64)
    return lists[np.arange(k) % 512 // 64]


def pack_weight(w):
    k, n = w.shape
    w = f64(np.asarray(w, np.float32).astype(ml_dtypes.bfloat16)).reshape(k // 32, 32, n)
    amax = np.abs(w).max(1)
    byte = np.clip(np.where(amax > 0, np.frexp(amax)[1] - 1 + 127 - 7, 1), 1, 254)
    scaled = (w * np.exp2(127.0 - byte)[:, None, :]).reshape(k, n).astype(np.float32)
    words = np.ascontiguousarray(scaled.reshape(k // 512, 128, 4, n).transpose(0, 1, 3, 2)).astype(ml_dtypes.float8_e4m3fn).view(np.uint8)
    return words, np.ascontiguousarray(byte.astype(np.uint8).reshape(k // 512, 16, n))


def unpack_weight(words, scales):
    g, p, n, _ = words.shape
    vals = np.ascontiguousarray(words).view(ml_dtypes.float8_e4m3fn).astype(np.float64) * np.repeat(np.exp2(scales.astype(np.float64) - 127.0), 8, axis=1)[..., None]
    return vals.transpose(0, 1, 3, 2).reshape(g * 512, n)


def sigmoid(v):
    return 1.0 / (1.0 + np.exp(-np.maximum(v, -700.0)))

def planes(y):
    n, m = y.shape
    v = y.astype(np.float32).astype(ml_dtypes.bfloat16).astype(np.float64).reshape(n // 32, 32, m)
    top = np.abs(v).max(1)
    byte = np.clip(np.where(top > 0, np.frexp(top)[1] - 1 + 127 - 7, 1), 1, 254)
    codes = (v * np.exp2(127.0 - byte)[:, None, :]).reshape(n, m).astype(np.float32).astype(ml_dtypes.float8_e4m3fn).view(np.uint8)
    words = codes.reshape(n // 512, 128, 4, m).transpose(0, 1, 3, 2)
    return np.ascontiguousarray(words), np.ascontiguousarray(byte.astype(np.uint8).reshape(n // 512, 16, m))


K, T, S, H, W, C = 512, 2048, 512, 512, 256, 512


def setup_inputs():
    n = np.random.standard_normal
    s = mx_kscale(K)[:, None]
    packed_xT = pack_weight(n((K, T)) * s)
    packed_w1 = pack_weight(n((K, H)) / np.sqrt(K) / s)
    perm = np.stack([np.random.permutation(S) for _ in range(8)])
    return {
        "x_words": packed_xT[0],
        "x_scales": packed_xT[1],
        "w1_words": packed_w1[0],
        "w1_scales": packed_w1[1],
        "gs": (np.random.uniform(0.5, 1.5, (K, 1)) / s).astype(np.float32),
        "offs": striped(np.random.permutation(T)[:S]),
        "n1": striped8(perm[:, :W]),
        "n2": striped8(perm[:, W:]),
        "n3": striped8(np.stack([np.random.permutation(S) for _ in range(8)])),
        "ca": striped(np.random.permutation(T)[:C]),
        "cb": striped(np.random.permutation(T)[:C]),
        "n4": striped8(np.stack([np.random.permutation(S) for _ in range(8)])),
        "n5": striped8(np.stack([np.random.permutation(S) for _ in range(8)])),
    }


def reference(x_words, x_scales, w1_words, w1_scales, gs, offs, n1, n2, n3, ca, cb, n4, n5):
    x_ca = unpack_weight(x_words, x_scales)[:, unstriped(ca)]
    xq = unpack_weight(x_words, x_scales)[:, unstriped(offs)]
    y = unpack_weight(w1_words, w1_scales).T @ xq
    pa = y[np.arange(H)[:, None], runs(n1, H)]
    pb = y[np.arange(H)[:, None], runs(n2, H)]
    ra = pa - (0.5 * pb)
    ds = y.copy()
    ds[np.arange(H)[:, None], runs(n2, H)] = ra
    z = f64(gs) * (ds - (0.5 * (ds[np.arange(H)[:, None], runs(n3, H)])))
    zq = mxq(z, 0, "e4m3")
    a = 0.0625 * (x_ca.T @ zq)
    x_cb = unpack_weight(x_words, x_scales)[:, unstriped(cb)]
    b = 0.0625 * (x_cb.T @ zq)
    out_0 = (a + a[np.arange(C)[:, None], runs(n4, C)]) * (sigmoid(b + b[np.arange(C)[:, None], runs(n5, C)]))
    return (out_0,) + planes(out_0)

@@ -1,0 +1,198 @@
+from contextlib import ExitStack
+
+import concourse.mybir as mybir
+
+F32 = mybir.dt.float32
+BF16 = mybir.dt.bfloat16
+I32 = mybir.dt.int32
+U32 = mybir.dt.uint32
+U16 = mybir.dt.uint16
+U8 = mybir.dt.uint8
+FP8X4 = mybir.dt.float8_e4m3fn_x4
+ACT = mybir.ActivationFunctionType
+ALU = mybir.AluOpType
+
+P = 128
+PACK = 4
+T = 2048
+S = 512
+HALF = 256
+CHUNKS = (256, 256)
+FUSED_A = (2, 3)
+FUSED_B = (0,)
+FLOPS = 3 * 2 * 512 * 512 * 512
+
+
+def tile_picked_ccmptriebfoldd_none_po_kernel(
+    tc, x_words, x_scales, w1_words, w1_scales, gs, offs, n1, n2, n3, ca, cb, n4, n5, out_0, out_1, out_2
+):
+    nc = tc.nc
+    with ExitStack() as ctx:
+        keep = ctx.enter_context(tc.tile_pool(name="keep", bufs=1))
+        psum = ctx.enter_context(tc.psum_pool(name="psum", bufs=1))
+
+        def load_list(src, name):
+            tile = keep.tile(list(src.shape), U16, name=name)
+            nc.sync.dma_start(tile[:], src)
+            return tile
+
+        def load_scale_rows(tile, src):
+            for q in range(4):
+                nc.sync.dma_start(
+                    tile[32 * q : 32 * q + 4, :].bitcast(I32), src[0, 4 * q : 4 * q + 4, :].bitcast(I32)
+                )
+
+        def dealt(ap):
+            return ap.rearrange("p (t m) -> p m t", t=PACK)
+
+        def half_cols(h):
+            return slice(h * HALF, (h + 1) * HALF)
+
+        def half_list(lst, h):
+            return lst[:, h * HALF // 16 : (h + 1) * HALF // 16]
+
+        xs = keep.tile([P, T], U8, align_bytes=64)
+        xw = keep.tile([P, T], U32, align_bytes=64)
+        w1s_raw = keep.tile([P, S], U8, align_bytes=64, tag="w1s_then_ca")
+        w1w_raw = keep.tile([P, S], U32, align_bytes=64)
+        nc.vector.memset(xs[:].bitcast(I32), 0)
+        nc.gpsimd.memset(w1s_raw[:].bitcast(I32), 0)
+
+        offs_l = load_list(offs, "offs_l")
+        ca_l = load_list(ca, "ca_l")
+        load_scale_rows(xs, x_scales)
+        nc.sync.dma_start(xw[:].bitcast(I32), x_words[0].rearrange("p n t -> p (n t)").bitcast(I32))
+        nc.sync.dma_start(w1w_raw[:].bitcast(I32), w1_words[0].rearrange("p n t -> p (n t)").bitcast(I32))
+        load_scale_rows(w1s_raw, w1_scales)
+        gs_t = keep.tile([P, PACK], F32)
+        nc.sync.dma_start(gs_t[:], gs.rearrange("(p t) o -> p (t o)", t=PACK))
+        n1_l = load_list(n1, "n1_l")
+        n2_l = load_list(n2, "n2_l")
+        n3_l = load_list(n3, "n3_l")
+        cb_l = load_list(cb, "cb_l")
+        n4_l = load_list(n4, "n4_l")
+        n5_l = load_list(n5, "n5_l")
+
+        xq_w = keep.tile([P, S], U32, align_bytes=64)
+        xq_s = keep.tile([P, S], U8, align_bytes=64)
+        ca_s = keep.tile([P, S], U8, align_bytes=64)
+        w1w = keep.tile([P, S], U32, align_bytes=64)
+        w1s = keep.tile([P, S], U8, align_bytes=64)
+
+        nc.scalar.copy(dealt(w1w[:]), w1w_raw[:].rearrange("p (m t) -> p m t", t=PACK))
+        nc.vector.tensor_copy(xq_s[:], xs[:].indirect(offs_l[:]))
+        nc.vector.tensor_copy(dealt(ca_s[:]), xs[:].indirect(ca_l[:]))
+        nc.vector.tensor_copy(dealt(w1s[:]), w1s_raw[:].rearrange("p (m t) -> p m t", t=PACK))
+        nc.vector.tensor_copy(xq_w[:], xw[:].indirect(offs_l[:]))
+        ca_w = keep.tile([P, S], U32, align_bytes=64, tag="w1s_then_ca")
+        nc.vector.tensor_copy(dealt(ca_w[:]), xw[:].indirect(ca_l[:]))
+
+        banks = [psum.tile([P, S], F32, name=f"bank{i}") for i in range(8)]
+
+        def product(bank, cols, lw, ls, t, rw, rs):
+            rows = slice(P * t, P * (t + 1))
+            nc.tensor.matmul_mx(
+                out=bank[:, cols], lhsT=lw[:, rows].bitcast(FP8X4), lhsT_scale=ls[:, rows],
+                rhs=rw[:, cols].bitcast(FP8X4), rhs_scale=rs[:, cols], start=True, stop=True,
+            )
+
+        ds = [keep.tile([P, S], F32, name=f"ds{t}") for t in range(PACK)]
+        for t in range(PACK):
+            product(banks[t], slice(0, S), w1w, w1s, t, xq_w, xq_s)
+        for t in range(PACK):
+            pa = keep.tile([P, HALF], F32, name=f"pa{t}")
+            pb = keep.tile([P, HALF], F32, name=f"pb{t}")
+            nc.scalar.activation(ds[t][:], banks[t][:], ACT.Copy, scale=gs_t[:, t : t + 1])
+            nc.scalar.activation(pa[:], ds[t][:].indirect(n1_l[:]), ACT.Copy)
+            if t in (0,):
+                nc.vector.tensor_scalar(pb[:], ds[t][:].indirect(n2_l[:]), -0.5, 0.0, ALU.mult, ALU.add)
+            else:
+                nc.scalar.activation(pb[:], ds[t][:].indirect(n2_l[:]), ACT.Copy, scale=-0.5)
+            nc.vector.tensor_tensor(ds[t][:].indirect(n2_l[:]), pa[:], pb[:], ALU.add)
+
+        z_w = keep.tile([P, S], U32, align_bytes=64)
+        z_s = keep.tile([P, S], U8, align_bytes=64)
+        for h in range(2):
+            cols = half_cols(h)
+            z_rows = keep.tile([P, PACK, HALF], BF16, name=f"z_rows{h}", align_bytes=64)
+            z_in = keep.tile([P, HALF, PACK], BF16, name=f"z_in{h}", align_bytes=64)
+            for t in range(PACK):
+                g3 = keep.tile([P, HALF], F32, name=f"g3_{h}_{t}", align_bytes=64)
+                nc.scalar.activation(g3[:], ds[t][:].indirect(half_list(n3_l, h)), ACT.Copy, scale=-0.5)
+                nc.vector.tensor_tensor(z_rows[:, t, :], ds[t][:, cols], g3[:], ALU.add)
+            nc.vector.tensor_copy(
+                z_in[:].rearrange("p (c i) t -> p c t i", i=4), z_rows[:].rearrange("p t (c i) -> p c t i", i=4)
+            )
+            nc.vector.quantize_mx(
+                out=z_w[:, cols].bitcast(FP8X4), scales=z_s[:, cols], in_=z_in[:].rearrange("p c t -> p (c t)")
+            )
+
+        a_sb = [keep.tile([P, S], F32, name=f"a{t}") for t in range(PACK)]
+        b_sb = [keep.tile([P, S], F32, name=f"b{t}") for t in range(PACK)]
+        for h in range(2):
+            cols = half_cols(h)
+            for t in range(PACK):
+                product(banks[4 + t], cols, ca_w, ca_s, t, z_w, z_s)
+                nc.scalar.activation(a_sb[t][:, cols], banks[4 + t][:, cols], ACT.Copy, scale=0.03125)
+
+        cb_s = keep.tile([P, S], U8, align_bytes=64, tag="z_in1")
+        cb_w = keep.tile([P, S], U32, align_bytes=64, tag="z_rows1")
+        nc.vector.tensor_copy(dealt(cb_s[:]), xs[:].indirect(cb_l[:]))
+        nc.vector.tensor_copy(dealt(cb_w[:]), xw[:].indirect(cb_l[:]))
+        for t in range(PACK):
+            product(banks[t], slice(0, S), cb_w, cb_s, t, z_w, z_s)
+
+        def second_copy(src, name):
+            again = keep.tile([P, S], F32, name=name)
+            nc.vector.tensor_copy(again[:], src[:])
+            return again
+
+        def sum_with_looked_up(dst, src, again, lst, cols, name):
+            part = lst[:, cols.start // 16 : cols.stop // 16]
+            if again is not None:
+                nc.vector.tensor_tensor(dst, src[:].indirect(part), again[:, cols], ALU.add)
+            else:
+                g = keep.tile([P, cols.stop - cols.start], F32, name=name)
+                nc.scalar.activation(g[:], src[:].indirect(part), ACT.Copy)
+                nc.vector.tensor_tensor(dst, src[:, cols], g[:], ALU.add)
+
+        u = [keep.tile([P, S], F32, name=f"u{t}") for t in range(PACK)]
+        a_again = [second_copy(a_sb[t], f"a_again{t}") if t in FUSED_A else None for t in range(PACK)]
+        for t in (0, 1):
+            for h in range(2):
+                sum_with_looked_up(u[t][:, half_cols(h)], a_sb[t], a_again[t], n4_l, half_cols(h), f"g4_{h}_{t}")
+        b_again = []
+        for t in range(PACK):
+            nc.scalar.activation(b_sb[t][:], banks[t][:], ACT.Copy, scale=0.03125)
+            b_again.append(second_copy(b_sb[t], f"b_again{t}") if t in FUSED_B else None)
+
+        out_rows = out_0.rearrange("(p t) j -> p t j", t=PACK)
+        o_w = keep.tile([P, S], U32, align_bytes=64)
+        o_s = keep.tile([P, S], U8, align_bytes=64)
+        first = 0
+        for c, width in enumerate(CHUNKS):
+            cols = slice(first, first + width)
+            first += width
+            o_rows = keep.tile([P, PACK, width], F32, name=f"o_rows{c}", align_bytes=64)
+            o_in = keep.tile([P, width, PACK], BF16, name=f"o_in{c}", align_bytes=64)
+            for t in range(PACK):
+                v = keep.tile([P, width], F32, name=f"v_{c}_{t}")
+                th = keep.tile([P, width], F32, name=f"th_{c}_{t}")
+                sum_with_looked_up(v[:], b_sb[t], b_again[t], n5_l, cols, f"g5_{c}_{t}")
+                if t not in (0, 1):
+                    sum_with_looked_up(u[t][:, cols], a_sb[t], a_again[t], n4_l, cols, f"g4c_{c}_{t}")
+                nc.scalar.activation(th[:], v[:], ACT.Tanh)
+                nc.vector.scalar_tensor_tensor(o_rows[:, t, :], th[:], 1.0, u[t][:, cols], ALU.add, ALU.mult)
+            nc.sync.dma_start(out_rows[:, :, cols], o_rows[:])
+            nc.vector.tensor_copy(
+                o_in[:].rearrange("p (c i) t -> p c t i", i=4), o_rows[:].rearrange("p t (c i) -> p c t i", i=4)
+            )
+            nc.vector.quantize_mx(
+                out=o_w[:, cols].bitcast(FP8X4), scales=o_s[:, cols], in_=o_in[:].rearrange("p c t -> p (c t)")
+            )
+            nc.sync.dma_start(
+                out_1[0].rearrange("p n t -> p (n t)").bitcast(I32)[:, cols], o_w[:, cols].bitcast(I32)
+            )
+        for q in range(4):
+            queue = nc.sync if q % 2 == 0 else nc.scalar
+            queue.dma_start(out_2[0, 4 * q : 4 * q + 4, :].bitcast(I32), o_s[32 * q : 32 * q + 4, :].bitcast(I32))

@@ -1,6 +1,7 @@
 from contextlib import ExitStack
 
 import concourse.mybir as mybir
+from concourse.masks import make_identity
 
 F32 = mybir.dt.float32
 BF16 = mybir.dt.bfloat16
@@ -17,9 +18,6 @@ PACK = 4
 T = 2048
 S = 512
 HALF = 256
-CHUNKS = (256, 256)
-FUSED_A = (2, 3)
-FUSED_B = (0,)
 FLOPS = 3 * 2 * 512 * 512 * 512
 
 
@@ -53,146 +51,209 @@ def tile_picked_ccmptriebfoldd_none_po_kernel(
 
         xs = keep.tile([P, T], U8, align_bytes=64)
         xw = keep.tile([P, T], U32, align_bytes=64)
-        w1s_raw = keep.tile([P, S], U8, align_bytes=64, tag="w1s_then_ca")
-        w1w_raw = keep.tile([P, S], U32, align_bytes=64)
+        w1s_raw = keep.tile([P, S], U8, align_bytes=64, tag="w1s_then_xq")
+        w1w_raw = keep.tile([P, S], U32, align_bytes=64, tag="w1w_then_cb")
         nc.vector.memset(xs[:].bitcast(I32), 0)
         nc.gpsimd.memset(w1s_raw[:].bitcast(I32), 0)
+        ident = keep.tile([P, P], F32)
+        make_identity(nc, ident[:])
 
         offs_l = load_list(offs, "offs_l")
-        ca_l = load_list(ca, "ca_l")
+        cb_l = load_list(cb, "cb_l")
         load_scale_rows(xs, x_scales)
         nc.sync.dma_start(xw[:].bitcast(I32), x_words[0].rearrange("p n t -> p (n t)").bitcast(I32))
-        nc.sync.dma_start(w1w_raw[:].bitcast(I32), w1_words[0].rearrange("p n t -> p (n t)").bitcast(I32))
         load_scale_rows(w1s_raw, w1_scales)
+        nc.sync.dma_start(w1w_raw[:].bitcast(I32), w1_words[0].rearrange("p n t -> p (n t)").bitcast(I32))
         gs_t = keep.tile([P, PACK], F32)
         nc.sync.dma_start(gs_t[:], gs.rearrange("(p t) o -> p (t o)", t=PACK))
         n1_l = load_list(n1, "n1_l")
         n2_l = load_list(n2, "n2_l")
         n3_l = load_list(n3, "n3_l")
-        cb_l = load_list(cb, "cb_l")
-        n4_l = load_list(n4, "n4_l")
+        ca_l = load_list(ca, "ca_l")
         n5_l = load_list(n5, "n5_l")
+        n4_l = load_list(n4, "n4_l")
 
-        xq_w = keep.tile([P, S], U32, align_bytes=64)
+        def in_order(ap):
+            return ap.rearrange("p (m t) -> p m t", t=PACK)
+
         xq_s = keep.tile([P, S], U8, align_bytes=64)
-        ca_s = keep.tile([P, S], U8, align_bytes=64)
+        cb_s_listed = keep.tile([P, S], U8, align_bytes=64)
         w1w = keep.tile([P, S], U32, align_bytes=64)
         w1s = keep.tile([P, S], U8, align_bytes=64)
 
-        nc.scalar.copy(dealt(w1w[:]), w1w_raw[:].rearrange("p (m t) -> p m t", t=PACK))
+        nc.scalar.copy(dealt(w1w[:]), in_order(w1w_raw[:]))
         nc.vector.tensor_copy(xq_s[:], xs[:].indirect(offs_l[:]))
-        nc.vector.tensor_copy(dealt(ca_s[:]), xs[:].indirect(ca_l[:]))
-        nc.vector.tensor_copy(dealt(w1s[:]), w1s_raw[:].rearrange("p (m t) -> p m t", t=PACK))
-        nc.vector.tensor_copy(xq_w[:], xw[:].indirect(offs_l[:]))
-        ca_w = keep.tile([P, S], U32, align_bytes=64, tag="w1s_then_ca")
-        nc.vector.tensor_copy(dealt(ca_w[:]), xw[:].indirect(ca_l[:]))
+        nc.vector.tensor_copy(cb_s_listed[:], xs[:].indirect(cb_l[:]))
+        nc.vector.tensor_copy(dealt(w1s[:]), in_order(w1s_raw[:]))
+        xq_w = [
+            keep.tile([P, HALF], U32, align_bytes=64, name="xq_w0"),
+            keep.tile([P, HALF], U32, align_bytes=64, name="xq_w1", tag="w1s_then_xq"),
+        ]
+        for h in range(2):
+            nc.vector.tensor_copy(xq_w[h][:], xw[:].indirect(half_list(offs_l, h)))
+        cb_s = keep.tile([P, S], U8, align_bytes=64, tag="w1s_then_xq")
+        cb_w = keep.tile([P, S], U32, align_bytes=64, tag="w1w_then_cb")
+        nc.vector.tensor_copy(dealt(cb_s[:]), in_order(cb_s_listed[:]))
+        nc.vector.tensor_copy(dealt(cb_w[:]), xw[:].indirect(cb_l[:]))
 
-        banks = [psum.tile([P, S], F32, name=f"bank{i}") for i in range(8)]
+        def bank(i, width=S):
+            return psum.tile([P, width], F32, name=f"bank{i}")
 
-        def product(bank, cols, lw, ls, t, rw, rs):
+        def product(dst, lw, ls, t, rw, rs):
             rows = slice(P * t, P * (t + 1))
             nc.tensor.matmul_mx(
-                out=bank[:, cols], lhsT=lw[:, rows].bitcast(FP8X4), lhsT_scale=ls[:, rows],
-                rhs=rw[:, cols].bitcast(FP8X4), rhs_scale=rs[:, cols], start=True, stop=True,
+                out=dst, lhsT=lw[:, rows].bitcast(FP8X4), lhsT_scale=ls[:, rows],
+                rhs=rw.bitcast(FP8X4), rhs_scale=rs, start=True, stop=True,
             )
 
         ds = [keep.tile([P, S], F32, name=f"ds{t}") for t in range(PACK)]
+        def make_y(t):
+            y = bank(t)
+            for h in range(2):
+                if t == 0 and h == 1:
+                    y = bank(4)
+                product(y[:, half_cols(h)], w1w, w1s, t, xq_w[h][:], xq_s[:, half_cols(h)])
+                if t == 0:
+                    nc.scalar.activation(
+                        ds[0][:, half_cols(h)], y[:, half_cols(h)], ACT.Copy, scale=gs_t[:, 0:1]
+                    )
+            if t > 0:
+                nc.scalar.activation(ds[t][:], y[:], ACT.Copy, scale=gs_t[:, t : t + 1])
+
+        make_y(0)
         for t in range(PACK):
-            product(banks[t], slice(0, S), w1w, w1s, t, xq_w, xq_s)
-        for t in range(PACK):
+            if t + 1 < PACK:
+                make_y(t + 1)
             pa = keep.tile([P, HALF], F32, name=f"pa{t}")
             pb = keep.tile([P, HALF], F32, name=f"pb{t}")
-            nc.scalar.activation(ds[t][:], banks[t][:], ACT.Copy, scale=gs_t[:, t : t + 1])
             nc.scalar.activation(pa[:], ds[t][:].indirect(n1_l[:]), ACT.Copy)
-            if t in (0,):
+            if t in (1,):
                 nc.vector.tensor_scalar(pb[:], ds[t][:].indirect(n2_l[:]), -0.5, 0.0, ALU.mult, ALU.add)
             else:
                 nc.scalar.activation(pb[:], ds[t][:].indirect(n2_l[:]), ACT.Copy, scale=-0.5)
             nc.vector.tensor_tensor(ds[t][:].indirect(n2_l[:]), pa[:], pb[:], ALU.add)
 
+        def weave(copy, dst, src):
+            copy(dst.rearrange("p (c i) t -> p c t i", i=4), src.rearrange("p t (c i) -> p c t i", i=4))
+
         z_w = keep.tile([P, S], U32, align_bytes=64)
         z_s = keep.tile([P, S], U8, align_bytes=64)
+        z_rows = [keep.tile([P, PACK, HALF], BF16, name=f"z_rows{h}", align_bytes=64) for h in range(2)]
+        for h, t in ((0,0),(0,1),(0,2),(1,0),(0,3),(1,1),(1,2),(1,3)):
+            cols = half_cols(h)
+            g3 = keep.tile([P, HALF], F32, name=f"g3_{h}_{t}", align_bytes=64)
+            nc.scalar.activation(g3[:], ds[t][:].indirect(half_list(n3_l, h)), ACT.Copy, scale=-0.5)
+            nc.vector.tensor_tensor(z_rows[h][:, t, :], ds[t][:, cols], g3[:], ALU.add)
+            if t == PACK - 1:
+                z_in = keep.tile([P, HALF, PACK], BF16, name=f"z_in{h}", align_bytes=64)
+                cut = HALF - 64 * h
+                weave(nc.vector.tensor_copy, z_in[:, :cut, :], z_rows[h][:, :, :cut])
+                if cut < HALF:
+                    weave(nc.scalar.copy, z_in[:, cut:, :], z_rows[h][:, :, cut:])
+                nc.vector.quantize_mx(
+                    out=z_w[:, cols].bitcast(FP8X4), scales=z_s[:, cols], in_=z_in[:].rearrange("p c t -> p (c t)")
+                )
+
+        b_sb = [keep.tile([P, S], F32, name=f"b{t}") for t in range(PACK)]
+        b_banks = [bank(4 + t) for t in range(PACK)]
         for h in range(2):
             cols = half_cols(h)
-            z_rows = keep.tile([P, PACK, HALF], BF16, name=f"z_rows{h}", align_bytes=64)
-            z_in = keep.tile([P, HALF, PACK], BF16, name=f"z_in{h}", align_bytes=64)
             for t in range(PACK):
-                g3 = keep.tile([P, HALF], F32, name=f"g3_{h}_{t}", align_bytes=64)
-                nc.scalar.activation(g3[:], ds[t][:].indirect(half_list(n3_l, h)), ACT.Copy, scale=-0.5)
-                nc.vector.tensor_tensor(z_rows[:, t, :], ds[t][:, cols], g3[:], ALU.add)
-            nc.vector.tensor_copy(
-                z_in[:].rearrange("p (c i) t -> p c t i", i=4), z_rows[:].rearrange("p t (c i) -> p c t i", i=4)
-            )
-            nc.vector.quantize_mx(
-                out=z_w[:, cols].bitcast(FP8X4), scales=z_s[:, cols], in_=z_in[:].rearrange("p c t -> p (c t)")
-            )
+                product(b_banks[t][:, cols], cb_w, cb_s, t, z_w[:, cols], z_s[:, cols])
+                nc.scalar.activation(b_sb[t][:, cols], b_banks[t][:, cols], ACT.Copy, scale=0.03125)
+
+        ca_s = keep.tile([P, S], U8, align_bytes=64, tag="w1s_then_ca")
+        ca_w = keep.tile([P, S], U32, align_bytes=64, tag="z_rows1")
+        nc.vector.tensor_copy(dealt(ca_w[:]), xw[:].indirect(ca_l[:]))
+        nc.vector.tensor_copy(dealt(ca_s[:]), xs[:].indirect(ca_l[:]))
+
+        def gate_turned(h, t):
+            g5 = keep.tile([P, HALF], F32, name=f"g5_{h}_{t}")
+            looked_up = b_sb[t][:].indirect(half_list(n5_l, h))
+            if (h, t) in ((0, 0), (1, 0)):
+                nc.vector.tensor_copy(g5[:], looked_up)
+            else:
+                nc.scalar.activation(g5[:], looked_up, ACT.Copy)
+            if (h, t) in ():
+                v = keep.tile([P, HALF], F32, name=f"v_{h}_{t}")
+                nc.vector.tensor_tensor(v[:], g5[:], b_sb[t][:, half_cols(h)], ALU.add)
+                th_plain = keep.tile([P, HALF], F32, name=f"th_{h}_{t}")
+                nc.scalar.activation(th_plain[:], v[:], ACT.Tanh)
+                return th_plain
+            turned = bank(4 + t, HALF)
+            for j in range(0, HALF, P):
+                own = b_sb[t][:, h * HALF + j : h * HALF + j + P]
+                nc.tensor.matmul(turned[:, j : j + P], own, ident[:], start=(j == 0), stop=False, is_transpose=True)
+            for j in range(0, HALF, P):
+                nc.tensor.matmul(
+                    turned[:, j : j + P], g5[:, j : j + P], ident[:], start=False, stop=(j + P == HALF), is_transpose=True
+                )
+            th_turned = keep.tile([P, HALF], F32, name=f"th_{h}_{t}")
+            nc.scalar.activation(th_turned[:], turned[:], ACT.Tanh)
+            return th_turned
 
         a_sb = [keep.tile([P, S], F32, name=f"a{t}") for t in range(PACK)]
-        b_sb = [keep.tile([P, S], F32, name=f"b{t}") for t in range(PACK)]
-        for h in range(2):
-            cols = half_cols(h)
-            for t in range(PACK):
-                product(banks[4 + t], cols, ca_w, ca_s, t, z_w, z_s)
-                nc.scalar.activation(a_sb[t][:, cols], banks[4 + t][:, cols], ACT.Copy, scale=0.03125)
+        a_again = {t: keep.tile([P, S], F32, name=f"a_again{t}") for t in range(PACK)}
 
-        cb_s = keep.tile([P, S], U8, align_bytes=64, tag="z_in1")
-        cb_w = keep.tile([P, S], U32, align_bytes=64, tag="z_rows1")
-        nc.vector.tensor_copy(dealt(cb_s[:]), xs[:].indirect(cb_l[:]))
-        nc.vector.tensor_copy(dealt(cb_w[:]), xw[:].indirect(cb_l[:]))
-        for t in range(PACK):
-            product(banks[t], slice(0, S), cb_w, cb_s, t, z_w, z_s)
-
-        def second_copy(src, name):
-            again = keep.tile([P, S], F32, name=name)
-            nc.vector.tensor_copy(again[:], src[:])
-            return again
-
-        def sum_with_looked_up(dst, src, again, lst, cols, name):
-            part = lst[:, cols.start // 16 : cols.stop // 16]
-            if again is not None:
-                nc.vector.tensor_tensor(dst, src[:].indirect(part), again[:, cols], ALU.add)
+        def make_a(t):
+            a = bank(t)
+            product(a[:], ca_w, ca_s, t, z_w[:], z_s[:])
+            nc.scalar.activation(a_sb[t][:], a[:], ACT.Copy, scale=0.03125)
+            if t in (0, 1):
+                nc.vector.tensor_copy(a_again[t][:], a_sb[t][:])
             else:
-                g = keep.tile([P, cols.stop - cols.start], F32, name=name)
-                nc.scalar.activation(g[:], src[:].indirect(part), ACT.Copy)
-                nc.vector.tensor_tensor(dst, src[:, cols], g[:], ALU.add)
-
-        u = [keep.tile([P, S], F32, name=f"u{t}") for t in range(PACK)]
-        a_again = [second_copy(a_sb[t], f"a_again{t}") if t in FUSED_A else None for t in range(PACK)]
-        for t in (0, 1):
-            for h in range(2):
-                sum_with_looked_up(u[t][:, half_cols(h)], a_sb[t], a_again[t], n4_l, half_cols(h), f"g4_{h}_{t}")
-        b_again = []
-        for t in range(PACK):
-            nc.scalar.activation(b_sb[t][:], banks[t][:], ACT.Copy, scale=0.03125)
-            b_again.append(second_copy(b_sb[t], f"b_again{t}") if t in FUSED_B else None)
+                nc.sync.dma_start(a_again[t][:], a_sb[t][:])
 
         out_rows = out_0.rearrange("(p t) j -> p t j", t=PACK)
+        o_rows = [keep.tile([P, PACK, HALF], F32, name=f"o_rows{h}", align_bytes=64) for h in range(2)]
+
+        def finish(h, t, th_turned):
+            cols = half_cols(h)
+            u = keep.tile([P, HALF], F32, name=f"u_{h}_{t}")
+            if (h, t) in ():
+                g4 = keep.tile([P, HALF], F32, name=f"g4_{h}_{t}")
+                nc.scalar.activation(g4[:], a_sb[t][:].indirect(half_list(n4_l, h)), ACT.Copy)
+                nc.vector.tensor_tensor(u[:], g4[:], a_sb[t][:, cols], ALU.add)
+            else:
+                nc.vector.tensor_tensor(u[:], a_sb[t][:].indirect(half_list(n4_l, h)), a_again[t][:, cols], ALU.add)
+            if (h, t) in ():
+                th = th_turned
+            else:
+                th = bank(t, HALF)
+                for j in range(0, HALF, P):
+                    nc.tensor.transpose(th[:, j : j + P], th_turned[:, j : j + P], ident[:])
+            nc.vector.scalar_tensor_tensor(o_rows[h][:, t, :], th[:], 1.0, u[:], ALU.add, ALU.mult)
+            nc.sync.dma_start(out_rows[:, t, cols], o_rows[h][:, t, :])
+
         o_w = keep.tile([P, S], U32, align_bytes=64)
         o_s = keep.tile([P, S], U8, align_bytes=64)
-        first = 0
-        for c, width in enumerate(CHUNKS):
-            cols = slice(first, first + width)
-            first += width
-            o_rows = keep.tile([P, PACK, width], F32, name=f"o_rows{c}", align_bytes=64)
-            o_in = keep.tile([P, width, PACK], BF16, name=f"o_in{c}", align_bytes=64)
-            for t in range(PACK):
-                v = keep.tile([P, width], F32, name=f"v_{c}_{t}")
-                th = keep.tile([P, width], F32, name=f"th_{c}_{t}")
-                sum_with_looked_up(v[:], b_sb[t], b_again[t], n5_l, cols, f"g5_{c}_{t}")
-                if t not in (0, 1):
-                    sum_with_looked_up(u[t][:, cols], a_sb[t], a_again[t], n4_l, cols, f"g4c_{c}_{t}")
-                nc.scalar.activation(th[:], v[:], ACT.Tanh)
-                nc.vector.scalar_tensor_tensor(o_rows[:, t, :], th[:], 1.0, u[t][:, cols], ALU.add, ALU.mult)
-            nc.sync.dma_start(out_rows[:, :, cols], o_rows[:])
-            nc.vector.tensor_copy(
-                o_in[:].rearrange("p (c i) t -> p c t i", i=4), o_rows[:].rearrange("p t (c i) -> p c t i", i=4)
-            )
+
+        def planes(h, on_scalar):
+            cols = half_cols(h)
+            o_in = keep.tile([P, HALF, PACK], BF16, name=f"o_in{h}", align_bytes=64)
+            cut = HALF - on_scalar
+            if cut > 0:
+                weave(nc.vector.tensor_copy, o_in[:, :cut, :], o_rows[h][:, :, :cut])
+            if on_scalar > 0:
+                weave(nc.scalar.copy, o_in[:, cut:, :], o_rows[h][:, :, cut:])
             nc.vector.quantize_mx(
                 out=o_w[:, cols].bitcast(FP8X4), scales=o_s[:, cols], in_=o_in[:].rearrange("p c t -> p (c t)")
             )
             nc.sync.dma_start(
                 out_1[0].rearrange("p n t -> p (n t)").bitcast(I32)[:, cols], o_w[:, cols].bitcast(I32)
             )
+
+        for t in range(PACK):
+            make_a(t)
+        gates = [gate_turned(0, t) for t in range(PACK)]
+        later = {}
+        for t in range(PACK):
+            finish(0, t, gates[t])
+            later[t] = gate_turned(1, t)
+        planes(0, 128)
+        for t in range(PACK):
+            finish(1, t, later[t])
+        planes(1, 96)
         for q in range(4):
             queue = nc.sync if q % 2 == 0 else nc.scalar
             queue.dma_start(out_2[0, 4 * q : 4 * q + 4, :].bitcast(I32), o_s[32 * q : 32 * q + 4, :].bitcast(I32))

@@ -17,8 +17,15 @@ P = 128
 PACK = 4
 T = 2048
 S = 512
-HALF = 256
+HALF = S // 2
+SCORE_SCALE = 0.0625 / 2
 FLOPS = 3 * 2 * 512 * 512 * 512
+
+N2_TILE_ON_VECTOR = 1
+B_FUSED_TILES = (0,)
+B_TURNED_TILES = (2, 3)
+A_COPIED_BY_VECTOR = (0, 1)
+WOVEN_BY_SCALAR = (256, 96)
 
 
 def tile_picked_ccmptriebfoldd_none_po_kernel(
@@ -34,20 +41,47 @@ def tile_picked_ccmptriebfoldd_none_po_kernel(
             nc.sync.dma_start(tile[:], src)
             return tile
 
-        def load_scale_rows(tile, src):
+        def load_scale_rows(tile, src, queues):
             for q in range(4):
-                nc.sync.dma_start(
+                queues[q % len(queues)].dma_start(
                     tile[32 * q : 32 * q + 4, :].bitcast(I32), src[0, 4 * q : 4 * q + 4, :].bitcast(I32)
                 )
 
+        def as_words(packed):
+            return packed[0].rearrange("p n t -> p (n t)").bitcast(I32)
+
         def dealt(ap):
             return ap.rearrange("p (t m) -> p m t", t=PACK)
+
+        def in_order(ap):
+            return ap.rearrange("p (m t) -> p m t", t=PACK)
 
         def half_cols(h):
             return slice(h * HALF, (h + 1) * HALF)
 
         def half_list(lst, h):
             return lst[:, h * HALF // 16 : (h + 1) * HALF // 16]
+
+        def bank(i, width=S):
+            return psum.tile([P, width], F32, name=f"bank{i}")
+
+        def product(dst, stat_words, stat_scales, t, mov_words, mov_scales):
+            rows = slice(P * t, P * (t + 1))
+            nc.tensor.matmul_mx(
+                out=dst,
+                lhsT=stat_words[:, rows].bitcast(FP8X4),
+                lhsT_scale=stat_scales[:, rows],
+                rhs=mov_words.bitcast(FP8X4),
+                rhs_scale=mov_scales,
+                start=True,
+                stop=True,
+            )
+
+        def weave(copy, dst, src):
+            copy(dst.rearrange("p (c i) t -> p c t i", i=4), src.rearrange("p t (c i) -> p c t i", i=4))
+
+        def quantize(words, scales, woven):
+            nc.vector.quantize_mx(out=words.bitcast(FP8X4), scales=scales, in_=woven.rearrange("p c t -> p (c t)"))
 
         xs = keep.tile([P, T], U8, align_bytes=64)
         xw = keep.tile([P, T], U32, align_bytes=64)
@@ -60,10 +94,10 @@ def tile_picked_ccmptriebfoldd_none_po_kernel(
 
         offs_l = load_list(offs, "offs_l")
         cb_l = load_list(cb, "cb_l")
-        load_scale_rows(xs, x_scales)
-        nc.sync.dma_start(xw[:].bitcast(I32), x_words[0].rearrange("p n t -> p (n t)").bitcast(I32))
-        load_scale_rows(w1s_raw, w1_scales)
-        nc.sync.dma_start(w1w_raw[:].bitcast(I32), w1_words[0].rearrange("p n t -> p (n t)").bitcast(I32))
+        load_scale_rows(xs, x_scales, (nc.sync, nc.scalar))
+        nc.sync.dma_start(xw[:].bitcast(I32), as_words(x_words))
+        load_scale_rows(w1s_raw, w1_scales, (nc.sync,))
+        nc.sync.dma_start(w1w_raw[:].bitcast(I32), as_words(w1_words))
         gs_t = keep.tile([P, PACK], F32)
         nc.sync.dma_start(gs_t[:], gs.rearrange("(p t) o -> p (t o)", t=PACK))
         n1_l = load_list(n1, "n1_l")
@@ -73,17 +107,13 @@ def tile_picked_ccmptriebfoldd_none_po_kernel(
         n5_l = load_list(n5, "n5_l")
         n4_l = load_list(n4, "n4_l")
 
-        def in_order(ap):
-            return ap.rearrange("p (m t) -> p m t", t=PACK)
-
         xq_s = keep.tile([P, S], U8, align_bytes=64)
-        cb_s_listed = keep.tile([P, S], U8, align_bytes=64)
+        cb_s = keep.tile([P, S], U8, align_bytes=64)
         w1w = keep.tile([P, S], U32, align_bytes=64)
         w1s = keep.tile([P, S], U8, align_bytes=64)
-
         nc.scalar.copy(dealt(w1w[:]), in_order(w1w_raw[:]))
         nc.vector.tensor_copy(xq_s[:], xs[:].indirect(offs_l[:]))
-        nc.vector.tensor_copy(cb_s_listed[:], xs[:].indirect(cb_l[:]))
+        nc.vector.tensor_copy(dealt(cb_s[:]), xs[:].indirect(cb_l[:]))
         nc.vector.tensor_copy(dealt(w1s[:]), in_order(w1s_raw[:]))
         xq_w = [
             keep.tile([P, HALF], U32, align_bytes=64, name="xq_w0"),
@@ -91,169 +121,141 @@ def tile_picked_ccmptriebfoldd_none_po_kernel(
         ]
         for h in range(2):
             nc.vector.tensor_copy(xq_w[h][:], xw[:].indirect(half_list(offs_l, h)))
-        cb_s = keep.tile([P, S], U8, align_bytes=64, tag="w1s_then_xq")
         cb_w = keep.tile([P, S], U32, align_bytes=64, tag="w1w_then_cb")
-        nc.vector.tensor_copy(dealt(cb_s[:]), in_order(cb_s_listed[:]))
         nc.vector.tensor_copy(dealt(cb_w[:]), xw[:].indirect(cb_l[:]))
 
-        def bank(i, width=S):
-            return psum.tile([P, width], F32, name=f"bank{i}")
-
-        def product(dst, lw, ls, t, rw, rs):
-            rows = slice(P * t, P * (t + 1))
-            nc.tensor.matmul_mx(
-                out=dst, lhsT=lw[:, rows].bitcast(FP8X4), lhsT_scale=ls[:, rows],
-                rhs=rw.bitcast(FP8X4), rhs_scale=rs, start=True, stop=True,
-            )
-
         ds = [keep.tile([P, S], F32, name=f"ds{t}") for t in range(PACK)]
-        def make_y(t):
-            y = bank(t)
-            for h in range(2):
-                if t == 0 and h == 1:
-                    y = bank(4)
-                product(y[:, half_cols(h)], w1w, w1s, t, xq_w[h][:], xq_s[:, half_cols(h)])
-                if t == 0:
-                    nc.scalar.activation(
-                        ds[0][:, half_cols(h)], y[:, half_cols(h)], ACT.Copy, scale=gs_t[:, 0:1]
-                    )
-            if t > 0:
-                nc.scalar.activation(ds[t][:], y[:], ACT.Copy, scale=gs_t[:, t : t + 1])
 
-        make_y(0)
+        def copy_y(t, cols, y):
+            nc.scalar.activation(ds[t][:, cols], y[:, cols], ACT.Copy, scale=gs_t[:, t : t + 1])
+
+        def y_half(y, t, h):
+            product(y[:, half_cols(h)], w1w, w1s, t, xq_w[h][:], xq_s[:, half_cols(h)])
+
+        for h in range(2):
+            y = bank(PACK * h)
+            y_half(y, 0, h)
+            copy_y(0, half_cols(h), y)
         for t in range(PACK):
             if t + 1 < PACK:
-                make_y(t + 1)
+                y = bank(t + 1)
+                for h in range(2):
+                    y_half(y, t + 1, h)
+                copy_y(t + 1, slice(0, S), y)
             pa = keep.tile([P, HALF], F32, name=f"pa{t}")
             pb = keep.tile([P, HALF], F32, name=f"pb{t}")
             nc.scalar.activation(pa[:], ds[t][:].indirect(n1_l[:]), ACT.Copy)
-            if t in (1,):
+            if t == N2_TILE_ON_VECTOR:
                 nc.vector.tensor_scalar(pb[:], ds[t][:].indirect(n2_l[:]), -0.5, 0.0, ALU.mult, ALU.add)
             else:
                 nc.scalar.activation(pb[:], ds[t][:].indirect(n2_l[:]), ACT.Copy, scale=-0.5)
             nc.vector.tensor_tensor(ds[t][:].indirect(n2_l[:]), pa[:], pb[:], ALU.add)
 
-        def weave(copy, dst, src):
-            copy(dst.rearrange("p (c i) t -> p c t i", i=4), src.rearrange("p t (c i) -> p c t i", i=4))
-
         z_w = keep.tile([P, S], U32, align_bytes=64)
         z_s = keep.tile([P, S], U8, align_bytes=64)
         z_rows = [keep.tile([P, PACK, HALF], BF16, name=f"z_rows{h}", align_bytes=64) for h in range(2)]
-        for h, t in ((0,0),(0,1),(0,2),(1,0),(0,3),(1,1),(1,2),(1,3)):
+        pieces = [(h, t) for h in range(2) for t in range(PACK)]
+        pieces[PACK - 1], pieces[PACK] = pieces[PACK], pieces[PACK - 1]
+        for h, t in pieces:
             cols = half_cols(h)
-            g3 = keep.tile([P, HALF], F32, name=f"g3_{h}_{t}", align_bytes=64)
+            g3 = keep.tile([P, HALF], F32, name=f"g3_{h}_{t}")
             nc.scalar.activation(g3[:], ds[t][:].indirect(half_list(n3_l, h)), ACT.Copy, scale=-0.5)
             nc.vector.tensor_tensor(z_rows[h][:, t, :], ds[t][:, cols], g3[:], ALU.add)
             if t == PACK - 1:
-                z_in = keep.tile([P, HALF, PACK], BF16, name=f"z_in{h}", align_bytes=64)
-                cut = HALF - 64 * h
-                weave(nc.vector.tensor_copy, z_in[:, :cut, :], z_rows[h][:, :, :cut])
-                if cut < HALF:
-                    weave(nc.scalar.copy, z_in[:, cut:, :], z_rows[h][:, :, cut:])
-                nc.vector.quantize_mx(
-                    out=z_w[:, cols].bitcast(FP8X4), scales=z_s[:, cols], in_=z_in[:].rearrange("p c t -> p (c t)")
-                )
+                z_woven = keep.tile([P, HALF, PACK], BF16, name=f"z_woven{h}", align_bytes=64)
+                weave(nc.vector.tensor_copy, z_woven[:], z_rows[h][:])
+                quantize(z_w[:, cols], z_s[:, cols], z_woven[:])
 
         b_sb = [keep.tile([P, S], F32, name=f"b{t}") for t in range(PACK)]
-        b_banks = [bank(4 + t) for t in range(PACK)]
+        b_banks = [bank(PACK + t) for t in range(PACK)]
         for h in range(2):
             cols = half_cols(h)
             for t in range(PACK):
                 product(b_banks[t][:, cols], cb_w, cb_s, t, z_w[:, cols], z_s[:, cols])
-                nc.scalar.activation(b_sb[t][:, cols], b_banks[t][:, cols], ACT.Copy, scale=0.03125)
+                nc.scalar.activation(b_sb[t][:, cols], b_banks[t][:, cols], ACT.Copy, scale=SCORE_SCALE)
 
-        ca_s = keep.tile([P, S], U8, align_bytes=64, tag="w1s_then_ca")
+        ca_s = keep.tile([P, S], U8, align_bytes=64)
         ca_w = keep.tile([P, S], U32, align_bytes=64, tag="z_rows1")
         nc.vector.tensor_copy(dealt(ca_w[:]), xw[:].indirect(ca_l[:]))
         nc.vector.tensor_copy(dealt(ca_s[:]), xs[:].indirect(ca_l[:]))
 
-        def gate_turned(h, t):
-            g5 = keep.tile([P, HALF], F32, name=f"g5_{h}_{t}")
-            looked_up = b_sb[t][:].indirect(half_list(n5_l, h))
-            if (h, t) in ((0, 0), (1, 0)):
-                nc.vector.tensor_copy(g5[:], looked_up)
-            else:
-                nc.scalar.activation(g5[:], looked_up, ACT.Copy)
-            if (h, t) in ():
-                v = keep.tile([P, HALF], F32, name=f"v_{h}_{t}")
-                nc.vector.tensor_tensor(v[:], g5[:], b_sb[t][:, half_cols(h)], ALU.add)
-                th_plain = keep.tile([P, HALF], F32, name=f"th_{h}_{t}")
-                nc.scalar.activation(th_plain[:], v[:], ACT.Tanh)
-                return th_plain
-            turned = bank(4 + t, HALF)
-            for j in range(0, HALF, P):
-                own = b_sb[t][:, h * HALF + j : h * HALF + j + P]
-                nc.tensor.matmul(turned[:, j : j + P], own, ident[:], start=(j == 0), stop=False, is_transpose=True)
-            for j in range(0, HALF, P):
-                nc.tensor.matmul(
-                    turned[:, j : j + P], g5[:, j : j + P], ident[:], start=False, stop=(j + P == HALF), is_transpose=True
-                )
-            th_turned = keep.tile([P, HALF], F32, name=f"th_{h}_{t}")
-            nc.scalar.activation(th_turned[:], turned[:], ACT.Tanh)
-            return th_turned
-
         a_sb = [keep.tile([P, S], F32, name=f"a{t}") for t in range(PACK)]
-        a_again = {t: keep.tile([P, S], F32, name=f"a_again{t}") for t in range(PACK)}
-
-        def make_a(t):
+        a_again = [keep.tile([P, S], F32, name=f"a_again{t}") for t in range(PACK)]
+        b_again = {t: keep.tile([P, S], F32, name=f"b_again{t}") for t in B_FUSED_TILES}
+        for t in range(PACK):
             a = bank(t)
             product(a[:], ca_w, ca_s, t, z_w[:], z_s[:])
-            nc.scalar.activation(a_sb[t][:], a[:], ACT.Copy, scale=0.03125)
-            if t in (0, 1):
+            nc.scalar.activation(a_sb[t][:], a[:], ACT.Copy, scale=SCORE_SCALE)
+            if t in A_COPIED_BY_VECTOR:
                 nc.vector.tensor_copy(a_again[t][:], a_sb[t][:])
             else:
                 nc.sync.dma_start(a_again[t][:], a_sb[t][:])
 
+        def gate(h, t):
+            cols = half_cols(h)
+            looked_up = b_sb[t][:].indirect(half_list(n5_l, h))
+            if t in B_FUSED_TILES:
+                if h == 0:
+                    nc.vector.tensor_copy(b_again[t][:], b_sb[t][:])
+                v = keep.tile([P, HALF], F32, name=f"v_{h}_{t}")
+                nc.vector.tensor_tensor(v[:], looked_up, b_again[t][:, cols], ALU.add)
+            else:
+                g5 = keep.tile([P, HALF], F32, name=f"g5_{h}_{t}")
+                nc.scalar.activation(g5[:], looked_up, ACT.Copy)
+                if t in B_TURNED_TILES:
+                    v = turned_sum(bank(PACK + t, HALF), b_sb[t][:, cols], g5[:])
+                else:
+                    v = keep.tile([P, HALF], F32, name=f"v_{h}_{t}")
+                    nc.vector.tensor_tensor(v[:], g5[:], b_sb[t][:, cols], ALU.add)
+            th = keep.tile([P, HALF], F32, name=f"th_{h}_{t}")
+            nc.scalar.activation(th[:], v[:], ACT.Tanh)
+            return th
+
+        def turned_sum(dst, first, second):
+            passes = [(src, j) for src in (first, second) for j in range(0, HALF, P)]
+            for i, (src, j) in enumerate(passes):
+                nc.tensor.matmul(
+                    dst[:, j : j + P], src[:, j : j + P], ident[:],
+                    start=(i == 0), stop=(i == len(passes) - 1), is_transpose=True,
+                )
+            return dst
+
         out_rows = out_0.rearrange("(p t) j -> p t j", t=PACK)
         o_rows = [keep.tile([P, PACK, HALF], F32, name=f"o_rows{h}", align_bytes=64) for h in range(2)]
 
-        def finish(h, t, th_turned):
+        def finish(h, t, th):
             cols = half_cols(h)
             u = keep.tile([P, HALF], F32, name=f"u_{h}_{t}")
-            if (h, t) in ():
-                g4 = keep.tile([P, HALF], F32, name=f"g4_{h}_{t}")
-                nc.scalar.activation(g4[:], a_sb[t][:].indirect(half_list(n4_l, h)), ACT.Copy)
-                nc.vector.tensor_tensor(u[:], g4[:], a_sb[t][:, cols], ALU.add)
-            else:
-                nc.vector.tensor_tensor(u[:], a_sb[t][:].indirect(half_list(n4_l, h)), a_again[t][:, cols], ALU.add)
-            if (h, t) in ():
-                th = th_turned
-            else:
-                th = bank(t, HALF)
+            nc.vector.tensor_tensor(u[:], a_sb[t][:].indirect(half_list(n4_l, h)), a_again[t][:, cols], ALU.add)
+            if t in B_TURNED_TILES:
+                turned, th = th, bank(t, HALF)
                 for j in range(0, HALF, P):
-                    nc.tensor.transpose(th[:, j : j + P], th_turned[:, j : j + P], ident[:])
+                    nc.tensor.transpose(th[:, j : j + P], turned[:, j : j + P], ident[:])
             nc.vector.scalar_tensor_tensor(o_rows[h][:, t, :], th[:], 1.0, u[:], ALU.add, ALU.mult)
             nc.sync.dma_start(out_rows[:, t, cols], o_rows[h][:, t, :])
 
         o_w = keep.tile([P, S], U32, align_bytes=64)
         o_s = keep.tile([P, S], U8, align_bytes=64)
 
-        def planes(h, on_scalar):
+        def quantize_out(h):
             cols = half_cols(h)
-            o_in = keep.tile([P, HALF, PACK], BF16, name=f"o_in{h}", align_bytes=64)
-            cut = HALF - on_scalar
+            o_woven = keep.tile([P, HALF, PACK], BF16, name=f"o_woven{h}", align_bytes=64)
+            cut = HALF - WOVEN_BY_SCALAR[h]
             if cut > 0:
-                weave(nc.vector.tensor_copy, o_in[:, :cut, :], o_rows[h][:, :, :cut])
-            if on_scalar > 0:
-                weave(nc.scalar.copy, o_in[:, cut:, :], o_rows[h][:, :, cut:])
-            nc.vector.quantize_mx(
-                out=o_w[:, cols].bitcast(FP8X4), scales=o_s[:, cols], in_=o_in[:].rearrange("p c t -> p (c t)")
-            )
-            nc.sync.dma_start(
-                out_1[0].rearrange("p n t -> p (n t)").bitcast(I32)[:, cols], o_w[:, cols].bitcast(I32)
-            )
+                weave(nc.vector.tensor_copy, o_woven[:, :cut, :], o_rows[h][:, :, :cut])
+            weave(nc.scalar.copy, o_woven[:, cut:, :], o_rows[h][:, :, cut:])
+            quantize(o_w[:, cols], o_s[:, cols], o_woven[:])
+            nc.sync.dma_start(as_words(out_1)[:, cols], o_w[:, cols].bitcast(I32))
 
+        first_gates = [gate(0, t) for t in range(PACK)]
+        second_gates = []
         for t in range(PACK):
-            make_a(t)
-        gates = [gate_turned(0, t) for t in range(PACK)]
-        later = {}
+            finish(0, t, first_gates[t])
+            second_gates.append(gate(1, t))
+        quantize_out(0)
         for t in range(PACK):
-            finish(0, t, gates[t])
-            later[t] = gate_turned(1, t)
-        planes(0, 128)
-        for t in range(PACK):
-            finish(1, t, later[t])
-        planes(1, 96)
+            finish(1, t, second_gates[t])
+        quantize_out(1)
         for q in range(4):
             queue = nc.sync if q % 2 == 0 else nc.scalar
             queue.dma_start(out_2[0, 4 * q : 4 * q + 4, :].bitcast(I32), o_s[32 * q : 32 * q + 4, :].bitcast(I32))

from contextlib import ExitStack

import concourse.mybir as mybir
from concourse.masks import make_identity

F32 = mybir.dt.float32
BF16 = mybir.dt.bfloat16
I32 = mybir.dt.int32
U32 = mybir.dt.uint32
U16 = mybir.dt.uint16
U8 = mybir.dt.uint8
FP8X4 = mybir.dt.float8_e4m3fn_x4
ACT = mybir.ActivationFunctionType
ALU = mybir.AluOpType

P = 128
PACK = 4
T = 2048
S = 512
HALF = S // 2
SCORE_SCALE = 0.0625 / 2
FLOPS = 3 * 2 * 512 * 512 * 512

N2_TILE_ON_VECTOR = 1
B_FUSED_TILES = (0,)
B_TURNED_TILES = (2, 3)
A_COPIED_BY_VECTOR = (0, 1)
WOVEN_BY_SCALAR = (256, 96)


def tile_picked_ccmptriebfoldd_none_po_kernel(
    tc, x_words, x_scales, w1_words, w1_scales, gs, offs, n1, n2, n3, ca, cb, n4, n5, out_0, out_1, out_2
):
    nc = tc.nc
    with ExitStack() as ctx:
        keep = ctx.enter_context(tc.tile_pool(name="keep", bufs=1))
        psum = ctx.enter_context(tc.psum_pool(name="psum", bufs=1))

        def load_list(src, name):
            tile = keep.tile(list(src.shape), U16, name=name)
            nc.sync.dma_start(tile[:], src)
            return tile

        def load_scale_rows(tile, src, queues):
            for q in range(4):
                queues[q % len(queues)].dma_start(
                    tile[32 * q : 32 * q + 4, :].bitcast(I32), src[0, 4 * q : 4 * q + 4, :].bitcast(I32)
                )

        def as_words(packed):
            return packed[0].rearrange("p n t -> p (n t)").bitcast(I32)

        def dealt(ap):
            return ap.rearrange("p (t m) -> p m t", t=PACK)

        def in_order(ap):
            return ap.rearrange("p (m t) -> p m t", t=PACK)

        def half_cols(h):
            return slice(h * HALF, (h + 1) * HALF)

        def half_list(lst, h):
            return lst[:, h * HALF // 16 : (h + 1) * HALF // 16]

        def bank(i, width=S):
            return psum.tile([P, width], F32, name=f"bank{i}")

        def product(dst, stat_words, stat_scales, t, mov_words, mov_scales):
            rows = slice(P * t, P * (t + 1))
            nc.tensor.matmul_mx(
                out=dst,
                lhsT=stat_words[:, rows].bitcast(FP8X4),
                lhsT_scale=stat_scales[:, rows],
                rhs=mov_words.bitcast(FP8X4),
                rhs_scale=mov_scales,
                start=True,
                stop=True,
            )

        def weave(copy, dst, src):
            copy(dst.rearrange("p (c i) t -> p c t i", i=4), src.rearrange("p t (c i) -> p c t i", i=4))

        def quantize(words, scales, woven):
            nc.vector.quantize_mx(out=words.bitcast(FP8X4), scales=scales, in_=woven.rearrange("p c t -> p (c t)"))

        xs = keep.tile([P, T], U8, align_bytes=64)
        xw = keep.tile([P, T], U32, align_bytes=64)
        w1s_raw = keep.tile([P, S], U8, align_bytes=64, tag="w1s_then_xq")
        w1w_raw = keep.tile([P, S], U32, align_bytes=64, tag="w1w_then_cb")
        nc.vector.memset(xs[:].bitcast(I32), 0)
        nc.gpsimd.memset(w1s_raw[:].bitcast(I32), 0)
        ident = keep.tile([P, P], F32)
        make_identity(nc, ident[:])

        offs_l = load_list(offs, "offs_l")
        cb_l = load_list(cb, "cb_l")
        load_scale_rows(xs, x_scales, (nc.sync, nc.scalar))
        nc.sync.dma_start(xw[:].bitcast(I32), as_words(x_words))
        load_scale_rows(w1s_raw, w1_scales, (nc.sync,))
        nc.sync.dma_start(w1w_raw[:].bitcast(I32), as_words(w1_words))
        gs_t = keep.tile([P, PACK], F32)
        nc.sync.dma_start(gs_t[:], gs.rearrange("(p t) o -> p (t o)", t=PACK))
        n1_l = load_list(n1, "n1_l")
        n2_l = load_list(n2, "n2_l")
        n3_l = load_list(n3, "n3_l")
        ca_l = load_list(ca, "ca_l")
        n5_l = load_list(n5, "n5_l")
        n4_l = load_list(n4, "n4_l")

        xq_s = keep.tile([P, S], U8, align_bytes=64)
        cb_s = keep.tile([P, S], U8, align_bytes=64)
        w1w = keep.tile([P, S], U32, align_bytes=64)
        w1s = keep.tile([P, S], U8, align_bytes=64)
        nc.scalar.copy(dealt(w1w[:]), in_order(w1w_raw[:]))
        nc.vector.tensor_copy(xq_s[:], xs[:].indirect(offs_l[:]))
        nc.vector.tensor_copy(dealt(cb_s[:]), xs[:].indirect(cb_l[:]))
        nc.vector.tensor_copy(dealt(w1s[:]), in_order(w1s_raw[:]))
        xq_w = [
            keep.tile([P, HALF], U32, align_bytes=64, name="xq_w0"),
            keep.tile([P, HALF], U32, align_bytes=64, name="xq_w1", tag="w1s_then_xq"),
        ]
        for h in range(2):
            nc.vector.tensor_copy(xq_w[h][:], xw[:].indirect(half_list(offs_l, h)))
        cb_w = keep.tile([P, S], U32, align_bytes=64, tag="w1w_then_cb")
        nc.vector.tensor_copy(dealt(cb_w[:]), xw[:].indirect(cb_l[:]))

        ds = [keep.tile([P, S], F32, name=f"ds{t}") for t in range(PACK)]

        def copy_y(t, cols, y):
            nc.scalar.activation(ds[t][:, cols], y[:, cols], ACT.Copy, scale=gs_t[:, t : t + 1])

        def y_half(y, t, h):
            product(y[:, half_cols(h)], w1w, w1s, t, xq_w[h][:], xq_s[:, half_cols(h)])

        for h in range(2):
            y = bank(PACK * h)
            y_half(y, 0, h)
            copy_y(0, half_cols(h), y)
        for t in range(PACK):
            if t + 1 < PACK:
                y = bank(t + 1)
                for h in range(2):
                    y_half(y, t + 1, h)
                copy_y(t + 1, slice(0, S), y)
            pa = keep.tile([P, HALF], F32, name=f"pa{t}")
            pb = keep.tile([P, HALF], F32, name=f"pb{t}")
            nc.scalar.activation(pa[:], ds[t][:].indirect(n1_l[:]), ACT.Copy)
            if t == N2_TILE_ON_VECTOR:
                nc.vector.tensor_scalar(pb[:], ds[t][:].indirect(n2_l[:]), -0.5, 0.0, ALU.mult, ALU.add)
            else:
                nc.scalar.activation(pb[:], ds[t][:].indirect(n2_l[:]), ACT.Copy, scale=-0.5)
            nc.vector.tensor_tensor(ds[t][:].indirect(n2_l[:]), pa[:], pb[:], ALU.add)

        z_w = keep.tile([P, S], U32, align_bytes=64)
        z_s = keep.tile([P, S], U8, align_bytes=64)
        z_rows = [keep.tile([P, PACK, HALF], BF16, name=f"z_rows{h}", align_bytes=64) for h in range(2)]
        pieces = [(h, t) for h in range(2) for t in range(PACK)]
        pieces[PACK - 1], pieces[PACK] = pieces[PACK], pieces[PACK - 1]
        for h, t in pieces:
            cols = half_cols(h)
            g3 = keep.tile([P, HALF], F32, name=f"g3_{h}_{t}")
            nc.scalar.activation(g3[:], ds[t][:].indirect(half_list(n3_l, h)), ACT.Copy, scale=-0.5)
            nc.vector.tensor_tensor(z_rows[h][:, t, :], ds[t][:, cols], g3[:], ALU.add)
            if t == PACK - 1:
                z_woven = keep.tile([P, HALF, PACK], BF16, name=f"z_woven{h}", align_bytes=64)
                weave(nc.vector.tensor_copy, z_woven[:], z_rows[h][:])
                quantize(z_w[:, cols], z_s[:, cols], z_woven[:])

        b_sb = [keep.tile([P, S], F32, name=f"b{t}") for t in range(PACK)]
        b_banks = [bank(PACK + t) for t in range(PACK)]
        for h in range(2):
            cols = half_cols(h)
            for t in range(PACK):
                product(b_banks[t][:, cols], cb_w, cb_s, t, z_w[:, cols], z_s[:, cols])
                nc.scalar.activation(b_sb[t][:, cols], b_banks[t][:, cols], ACT.Copy, scale=SCORE_SCALE)

        ca_s = keep.tile([P, S], U8, align_bytes=64)
        ca_w = keep.tile([P, S], U32, align_bytes=64, tag="z_rows1")
        nc.vector.tensor_copy(dealt(ca_w[:]), xw[:].indirect(ca_l[:]))
        nc.vector.tensor_copy(dealt(ca_s[:]), xs[:].indirect(ca_l[:]))

        a_sb = [keep.tile([P, S], F32, name=f"a{t}") for t in range(PACK)]
        a_again = [keep.tile([P, S], F32, name=f"a_again{t}") for t in range(PACK)]
        b_again = {t: keep.tile([P, S], F32, name=f"b_again{t}") for t in B_FUSED_TILES}
        for t in range(PACK):
            a = bank(t)
            product(a[:], ca_w, ca_s, t, z_w[:], z_s[:])
            nc.scalar.activation(a_sb[t][:], a[:], ACT.Copy, scale=SCORE_SCALE)
            if t in A_COPIED_BY_VECTOR:
                nc.vector.tensor_copy(a_again[t][:], a_sb[t][:])
            else:
                nc.sync.dma_start(a_again[t][:], a_sb[t][:])

        def gate(h, t):
            cols = half_cols(h)
            looked_up = b_sb[t][:].indirect(half_list(n5_l, h))
            if t in B_FUSED_TILES:
                if h == 0:
                    nc.vector.tensor_copy(b_again[t][:], b_sb[t][:])
                v = keep.tile([P, HALF], F32, name=f"v_{h}_{t}")
                nc.vector.tensor_tensor(v[:], looked_up, b_again[t][:, cols], ALU.add)
            else:
                g5 = keep.tile([P, HALF], F32, name=f"g5_{h}_{t}")
                nc.scalar.activation(g5[:], looked_up, ACT.Copy)
                if t in B_TURNED_TILES:
                    v = turned_sum(bank(PACK + t, HALF), b_sb[t][:, cols], g5[:])
                else:
                    v = keep.tile([P, HALF], F32, name=f"v_{h}_{t}")
                    nc.vector.tensor_tensor(v[:], g5[:], b_sb[t][:, cols], ALU.add)
            th = keep.tile([P, HALF], F32, name=f"th_{h}_{t}")
            nc.scalar.activation(th[:], v[:], ACT.Tanh)
            return th

        def turned_sum(dst, first, second):
            passes = [(src, j) for src in (first, second) for j in range(0, HALF, P)]
            for i, (src, j) in enumerate(passes):
                nc.tensor.matmul(
                    dst[:, j : j + P], src[:, j : j + P], ident[:],
                    start=(i == 0), stop=(i == len(passes) - 1), is_transpose=True,
                )
            return dst

        out_rows = out_0.rearrange("(p t) j -> p t j", t=PACK)
        o_rows = [keep.tile([P, PACK, HALF], F32, name=f"o_rows{h}", align_bytes=64) for h in range(2)]

        def finish(h, t, th):
            cols = half_cols(h)
            u = keep.tile([P, HALF], F32, name=f"u_{h}_{t}")
            nc.vector.tensor_tensor(u[:], a_sb[t][:].indirect(half_list(n4_l, h)), a_again[t][:, cols], ALU.add)
            if t in B_TURNED_TILES:
                turned, th = th, bank(t, HALF)
                for j in range(0, HALF, P):
                    nc.tensor.transpose(th[:, j : j + P], turned[:, j : j + P], ident[:])
            nc.vector.scalar_tensor_tensor(o_rows[h][:, t, :], th[:], 1.0, u[:], ALU.add, ALU.mult)
            nc.sync.dma_start(out_rows[:, t, cols], o_rows[h][:, t, :])

        o_w = keep.tile([P, S], U32, align_bytes=64)
        o_s = keep.tile([P, S], U8, align_bytes=64)

        def quantize_out(h):
            cols = half_cols(h)
            o_woven = keep.tile([P, HALF, PACK], BF16, name=f"o_woven{h}", align_bytes=64)
            cut = HALF - WOVEN_BY_SCALAR[h]
            if cut > 0:
                weave(nc.vector.tensor_copy, o_woven[:, :cut, :], o_rows[h][:, :, :cut])
            weave(nc.scalar.copy, o_woven[:, cut:, :], o_rows[h][:, :, cut:])
            quantize(o_w[:, cols], o_s[:, cols], o_woven[:])
            nc.sync.dma_start(as_words(out_1)[:, cols], o_w[:, cols].bitcast(I32))

        first_gates = [gate(0, t) for t in range(PACK)]
        second_gates = []
        for t in range(PACK):
            finish(0, t, first_gates[t])
            second_gates.append(gate(1, t))
        quantize_out(0)
        for t in range(PACK):
            finish(1, t, second_gates[t])
        quantize_out(1)
        for q in range(4):
            queue = nc.sync if q % 2 == 0 else nc.scalar
            queue.dma_start(out_2[0, 4 * q : 4 * q + 4, :].bitcast(I32), o_s[32 * q : 32 * q + 4, :].bitcast(I32))
